import numpy as np
import ml_dtypes


def mxq(x, axis, fmt="e4m3"):
    dtype, down = {"e4m3": (ml_dtypes.float8_e4m3fn, 7), "e5m2": (ml_dtypes.float8_e5m2, 14)}[fmt]
    v = np.moveaxis(np.asarray(x, np.float32).astype(ml_dtypes.bfloat16).astype(np.float64), axis, -1)
    blocks = v.reshape(v.shape[:-1] + (-1, 32))
    amax = np.abs(blocks).max(-1, keepdims=True)
    byte = np.maximum(np.where(amax > 0, np.frexp(amax)[1] - 1 + 127, 0) - down, 1)
    scale = np.exp2(byte - 127.0)
    codes = (blocks / scale).astype(np.float32).astype(dtype).astype(np.float64)
    return np.moveaxis((codes * scale).reshape(v.shape), -1, axis)


WIDE = False


def mx_kscale(k):
    if not WIDE:
        return np.ones(k)
    levels = np.array([10, -10, 5, -5, 0])
    if k % 512:
        return np.exp2(np.random.permutation(np.resize(levels, k // 32))).repeat(32)
    a = np.empty((k // 512, 16))
    for p in range(k // 512):
        a[p, :8] = np.random.permutation(np.resize(levels, 8))
        for g in range(8):
            far = levels[np.abs(levels - a[p, g]) >= 10]
            a[p, g + 8] = far[np.random.randint(len(far))]
    return np.exp2(a.ravel()).repeat(32)


def f64(x):
    return np.asarray(x).astype(np.float64)


def striped(idx):
    return np.tile(idx.reshape(-1, 16).T, (8, 1)).astype(np.uint16)


def unstriped(offs):
    return offs[:16].T.reshape(-1).astype(np.int64)


E2M1 = np.array([0.0, 0.5, 1.0, 1.5, 2.0, 3.0, 4.0, 6.0, -0.0, -0.5, -1.0, -1.5, -2.0, -3.0, -4.0, -6.0])


def pack_weight(w, fmt):
    k, n = w.shape
    w = f64(np.asarray(w, np.float32).astype(ml_dtypes.bfloat16)).reshape(k // 32, 32, n)
    amax = np.abs(w).max(1)
    if fmt == "e4m3":
        byte = np.frexp(amax)[1] - 1 + 127 - 7
    else:
        mant, ex = np.frexp(amax / 6.0)
        byte = np.where(mant > 0.5, ex, ex - 1) + 127
    byte = np.clip(np.where(amax > 0, byte, 1), 1, 254)
    scaled = (w * np.exp2(127.0 - byte)[:, None, :]).reshape(k, n).astype(np.float32)
    by_word = np.ascontiguousarray(scaled.reshape(k // 512, 128, 4, n).transpose(0, 1, 3, 2))
    if fmt == "e4m3":
        words = by_word.astype(ml_dtypes.float8_e4m3fn).view(np.uint8)
    else:
        c = by_word.astype(ml_dtypes.float4_e2m1fn).view(np.uint8) & 0xF
        words = (c[..., 0::2] | (c[..., 1::2] << 4)).reshape(k // 512, 128, 2 * n)
    return np.ascontiguousarray(words), np.ascontiguousarray(byte.astype(np.uint8).reshape(k // 512, 16, n))


def unpack_weight(words, scales, fmt):
    g, _, n = scales.shape
    words = np.ascontiguousarray(words).reshape(g, 128, n, -1)
    if fmt == "e4m3":
        vals = words.view(ml_dtypes.float8_e4m3fn).astype(np.float64)
    else:
        nib = np.empty((g, 128, n, 4), np.uint8)
        nib[..., 0::2] = words & 0xF
        nib[..., 1::2] = words >> 4
        vals = E2M1[nib]
    vals = vals * np.repeat(np.exp2(scales.astype(np.float64) - 127.0), 8, axis=1)[..., None]
    return vals.transpose(0, 1, 3, 2).reshape(g * 512, n)


def pack_table(v):
    words, scales = pack_weight(v, "e4m3")
    return np.concatenate([words.reshape(words.shape[0], -1), scales.reshape(scales.shape[0], -1)], axis=1)


def unpack_table(tab):
    g, t = tab.shape[0], tab.shape[1] // 528
    return unpack_weight(tab[:, :512 * t].reshape(g, 128, t, 4), tab[:, 512 * t:].reshape(g, 16, t), "e4m3")


K, M, T, S = 1536, 1024, 512, 256


def setup_inputs():
    n = np.random.standard_normal
    s = mx_kscale(K)[:, None]
    u = mx_kscale(512)[:, None]
    p_w4 = pack_weight(n((K, M)) / np.sqrt(K) / s, "e2m1")
    return {
        "tab": pack_table(n((K, T)) * s),
        "w4_words": p_w4[0],
        "w4_scales": p_w4[1],
        "down": (n((K, 512)) / np.sqrt(K) / s * u.T).astype(np.float32),
        "up": (0.5 * n((512, M)) / np.sqrt(512) / u).astype(np.float32),
        "wgo": np.tile(np.random.uniform(0.5, 2.0, S), (128, 1)).astype(np.float32),
        "offs": striped(np.random.permutation(T)[:S]),
        "offs2": striped(np.random.permutation(T)[:S]),
    }


def reference(tab, w4_words, w4_scales, down, up, wgo, offs, offs2):
    tab_ = unpack_table(tab)[:, unstriped(offs)]
    w4_ = unpack_weight(w4_words, w4_scales, "e2m1")
    down_ = mxq(f64(down), 0, "e4m3")
    up_ = mxq(f64(up), 0, "e4m3")
    h_ = mxq(down_.T @ tab_, 0, "e4m3")
    y = w4_.T @ tab_ + up_.T @ h_
    out = np.zeros((M, T))
    out[:, unstriped(offs2)] = f64(wgo)[0] * (y)
    return out

@@ -1,0 +1,214 @@
+from contextlib import ExitStack
+
+import concourse.mybir as mybir
+
+K, M, T, S, R = 1536, 1024, 512, 256, 512
+FLOPS = 2 * S * (K * R + K * M + R * M)
+
+F32 = mybir.dt.float32
+BF16 = mybir.dt.bfloat16
+I32 = mybir.dt.int32
+U32 = mybir.dt.uint32
+U16 = mybir.dt.uint16
+U8 = mybir.dt.uint8
+FP8X4 = mybir.dt.float8_e4m3fn_x4
+FP4X4 = mybir.dt.float4_e2m1fn_x4
+MULT = mybir.AluOpType.mult
+
+P = 128
+PACK = 4
+K_PASS = P * PACK
+PASSES = K // K_PASS
+HALF = S // 2
+N_TILES = M // P
+WINDOWS = 4
+UP_GROUPS = [(0, 1), (1, 2), (2, 4), (4, 8)]
+W4_GROUPS = [(0, 2), (2, 8)]
+
+
+def tile_list_tabscat_l_none_kernel(tc, tab, w4_words, w4_scales, down, up, wgo, offs, offs2, out):
+    nc = tc.nc
+    with ExitStack() as ctx:
+        keep = ctx.enter_context(tc.tile_pool(name="keep", bufs=1))
+        ring = ctx.enter_context(tc.tile_pool(name="ring", bufs=3))
+        psum_h = ctx.enter_context(tc.psum_pool(name="psum_h", bufs=1))
+        psum_y = ctx.enter_context(tc.psum_pool(name="psum_y", bufs=3))
+
+        pick = keep.tile([P, S // 16], U16, name="pick")
+        place = keep.tile([P, S // 16], U16, name="place")
+        nc.sync.dma_start(pick[:], offs)
+
+        tab_sc = keep.tile([P, PASSES, T], U8, name="tab_sc", align_bytes=64)
+        w4_sc = keep.tile([P, PASSES, M], U8, name="w4_sc", align_bytes=64)
+        nc.vector.memset(tab_sc[:].bitcast(I32), 0)
+        nc.vector.memset(w4_sc[:].bitcast(I32), 0)
+        tab_sc_rows = tab[:, K_PASS * T :].rearrange("a (q r t) -> r q a t", q=4, r=4)
+        for r in range(4):
+            nc.scalar.dma_start(tab_sc[r:P:32, :, :].bitcast(I32), tab_sc_rows[r].bitcast(I32))
+        windows = [keep.tile([P, T], F32, name="window%d" % i) for i in range(WINDOWS)]
+        for w in windows:
+            nc.vector.memset(w[:], 0.0)
+
+        down_raw = {}
+        tab_w = {}
+
+        def load_down(a):
+            for b in range(2):
+                t = keep.tile([P, PACK, R // 2], F32, name="down_raw%d_%d" % (a, b))
+                rows = down[a * K_PASS : (a + 1) * K_PASS, b * (R // 2) : (b + 1) * (R // 2)]
+                nc.sync.dma_start(t[:], rows.rearrange("(p j) c -> p j c", j=PACK))
+                down_raw[(a, b)] = t
+
+        def load_tab(a):
+            t = keep.tile([P, T], U32, name="tab_w%d" % a, align_bytes=64)
+            nc.sync.dma_start(t[:].bitcast(I32), tab[a, : K_PASS * T].rearrange("(p w) -> p w", p=P).bitcast(I32))
+            tab_w[a] = t
+
+        up_raw = {}
+
+        def load_up(lo, hi):
+            t = keep.tile([P, PACK, (hi - lo) * P], F32, name="up_raw%d" % lo)
+            nc.sync.dma_start(t[:], up[:, lo * P : hi * P].rearrange("(p j) c -> p j c", j=PACK))
+            for i in range(lo, hi):
+                up_raw[i] = t[:, :, (i - lo) * P : (i - lo + 1) * P]
+
+        w4_w = {}
+
+        def load_w4(lo, hi):
+            t = keep.tile([P, PASSES, (hi - lo) * 2 * P], U8, name="w4_w%d" % lo, align_bytes=64)
+            src = w4_words[:, :, lo * 2 * P : hi * 2 * P].rearrange("a p w -> p a w")
+            nc.sync.dma_start(t[:].bitcast(I32), src.bitcast(I32))
+            for i in range(lo, hi):
+                w4_w[i] = (t, (i - lo) * 2 * P)
+
+        load_down(0)
+        load_tab(0)
+        load_down(1)
+        load_tab(1)
+        load_tab(2)
+        load_down(2)
+        load_up(*UP_GROUPS[0])
+        w4_sc_rows = w4_scales.rearrange("a (q r) n -> r q a n", r=4)
+        for r in range(4):
+            nc.sync.dma_start(w4_sc[r:P:32, :, :].bitcast(I32), w4_sc_rows[r].bitcast(I32))
+        load_w4(*W4_GROUPS[0])
+        load_up(*UP_GROUPS[1])
+        weight = keep.tile([P, S], F32, name="weight")
+        nc.sync.dma_start(weight[:], wgo)
+        nc.sync.dma_start(place[:], offs2)
+        load_up(*UP_GROUPS[2])
+        load_w4(*W4_GROUPS[1])
+        load_up(*UP_GROUPS[3])
+
+        got_w = [keep.tile([P, S], U32, name="got_w%d" % a, align_bytes=64) for a in range(PASSES)]
+        got_sc = [keep.tile([P, S], U8, name="got_sc%d" % a, align_bytes=64) for a in range(PASSES)]
+        for a in range(PASSES):
+            nc.vector.tensor_copy(got_sc[a][:], tab_sc[:, a, :].indirect(pick[:]))
+
+        h_banks = [psum_h.tile([P, PACK, HALF], F32, name="h_bank%d" % b) for b in range(2)]
+        down_q = [keep.tile([P, R], U32, name="down_q%d" % a, align_bytes=64) for a in range(PASSES)]
+        down_sc = [keep.tile([P, R], U8, name="down_sc%d" % a, align_bytes=64) for a in range(PASSES)]
+
+        def weave_down(copy, dst, raw):
+            copy(dst.rearrange("p t m j -> p m j t"), raw.rearrange("p j (m t) -> p m j t", t=PACK))
+
+        def h_passes(a, t):
+            cols = slice(t * P, (t + 1) * P)
+            for b in range(2):
+                pos = slice(b * HALF, (b + 1) * HALF)
+                nc.tensor.matmul_mx(
+                    out=h_banks[b][:, t, :],
+                    lhsT=down_q[a][:, cols].bitcast(FP8X4),
+                    lhsT_scale=down_sc[a][:, cols],
+                    rhs=got_w[a][:, pos].bitcast(FP8X4),
+                    rhs_scale=got_sc[a][:, pos],
+                    start=(a == 0 and t == 0),
+                    stop=(a == PASSES - 1 and t == PACK - 1),
+                )
+
+        HM = P // 2
+        for a in range(PASSES - 1):
+            nc.vector.tensor_copy(got_w[a][:], tab_w[a][:].indirect(pick[:]))
+            woven = keep.tile([P, PACK, P, PACK], BF16, name="down_bf%d" % a, align_bytes=64)
+            for b in range(2):
+                weave_down(nc.scalar.copy, woven[:, :, b * HM : (b + 1) * HM, :], down_raw[(a, b)][:])
+            nc.vector.quantize_mx(
+                out=down_q[a][:].bitcast(FP8X4), scales=down_sc[a][:], in_=woven[:].rearrange("p t m j -> p (t m j)")
+            )
+            for t in range(PACK):
+                h_passes(a, t)
+        a = PASSES - 1
+        nc.vector.tensor_copy(got_w[a][:], tab_w[a][:].indirect(pick[:]))
+        halves = [keep.tile([P, PACK, HM, PACK], BF16, name="down_last%d" % b, align_bytes=64) for b in range(2)]
+        for b in range(2):
+            weave_down(nc.vector.tensor_copy, halves[b][:], down_raw[(a, b)][:])
+            for t in range(PACK):
+                cols = slice(t * P + b * HM, t * P + (b + 1) * HM)
+                nc.vector.quantize_mx(
+                    out=down_q[a][:, cols].bitcast(FP8X4),
+                    scales=down_sc[a][:, cols],
+                    in_=halves[b][:, t, :, :].rearrange("p m j -> p (m j)"),
+                )
+        for t in range(PACK):
+            h_passes(a, t)
+
+        up_q = {}
+
+        def weave_up(i):
+            woven = keep.tile([P, P, PACK], BF16, name="up_bf%d" % i, align_bytes=64)
+            nc.scalar.copy(
+                woven[:].rearrange("p (c i) j -> p c j i", i=4), up_raw[i].rearrange("p j (c i) -> p c j i", i=4)
+            )
+            codes = keep.tile([P, P], U32, name="up_q%d" % i, align_bytes=64)
+            scales = keep.tile([P, P], U8, name="up_sc%d" % i, align_bytes=64)
+            nc.vector.quantize_mx(
+                out=codes[:].bitcast(FP8X4), scales=scales[:], in_=woven[:].rearrange("p c j -> p (c j)")
+            )
+            up_q[i] = (codes, scales)
+
+        weave_up(0)
+
+        h_q = keep.tile([P, S], U32, name="h_q", align_bytes=64)
+        h_sc = keep.tile([P, S], U8, name="h_sc", align_bytes=64)
+        h_bf = [keep.tile([P, HALF, PACK], BF16, name="h_bf%d" % b, align_bytes=64) for b in range(2)]
+        nc.scalar.copy(h_bf[0][:], h_banks[0][:].rearrange("p t s -> p s t"))
+        nc.vector.tensor_copy(h_bf[1][:], h_banks[1][:].rearrange("p t s -> p s t"))
+        for b in range(2):
+            pos = slice(b * HALF, (b + 1) * HALF)
+            nc.vector.quantize_mx(
+                out=h_q[:, pos].bitcast(FP8X4), scales=h_sc[:, pos], in_=h_bf[b][:].rearrange("p s t -> p (s t)")
+            )
+
+        weave_up(1)
+        for i in range(N_TILES):
+            acc = psum_y.tile([P, S], F32, name="acc")
+            words, at = w4_w[i]
+            for a in range(PASSES):
+                for b in range(2):
+                    pos = slice(b * HALF, (b + 1) * HALF)
+                    nc.tensor.matmul_mx(
+                        out=acc[:, pos],
+                        lhsT=words[:, a, at : at + 2 * P].bitcast(FP4X4),
+                        lhsT_scale=w4_sc[:, a, i * P : (i + 1) * P],
+                        rhs=got_w[a][:, pos].bitcast(FP8X4),
+                        rhs_scale=got_sc[a][:, pos],
+                        start=(a == 0 and b == 0),
+                        stop=False,
+                    )
+            codes, scales = up_q[i]
+            nc.tensor.matmul_mx(
+                out=acc[:],
+                lhsT=codes[:].bitcast(FP8X4),
+                lhsT_scale=scales[:],
+                rhs=h_q[:].bitcast(FP8X4),
+                rhs_scale=h_sc[:],
+                start=False,
+                stop=True,
+            )
+            y = ring.tile([P, S], F32, name="y")
+            nc.scalar.copy(y[:], acc[:])
+            if i + 2 < N_TILES:
+                weave_up(i + 2)
+            window = windows[i % WINDOWS]
+            nc.vector.tensor_tensor(window[:].indirect(place[:]), y[:], weight[:], MULT)
+            nc.sync.dma_start(out[i * P : (i + 1) * P, :], window[:])

@@ -21,9 +21,10 @@ K_PASS = P * PACK
 PASSES = K // K_PASS
 HALF = S // 2
 N_TILES = M // P
-WINDOWS = 4
-UP_GROUPS = [(0, 1), (1, 2), (2, 4), (4, 8)]
-W4_GROUPS = [(0, 2), (2, 8)]
+WINDOWS = 6
+SCALAR_SHARE = 44
+UP_GROUPS = [(0, 1), (1, 2), (2, 3), (3, 5), (5, 8)]
+W4_GROUPS = [(0, 4), (4, 8)]
 
 
 def tile_list_tabscat_l_none_kernel(tc, tab, w4_words, w4_scales, down, up, wgo, offs, offs2, out):
@@ -32,7 +33,7 @@ def tile_list_tabscat_l_none_kernel(tc, tab, w4_words, w4_scales, down, up, wgo,
         keep = ctx.enter_context(tc.tile_pool(name="keep", bufs=1))
         ring = ctx.enter_context(tc.tile_pool(name="ring", bufs=3))
         psum_h = ctx.enter_context(tc.psum_pool(name="psum_h", bufs=1))
-        psum_y = ctx.enter_context(tc.psum_pool(name="psum_y", bufs=3))
+        psum_y = ctx.enter_context(tc.psum_pool(name="psum_y", bufs=2))
 
         pick = keep.tile([P, S // 16], U16, name="pick")
         place = keep.tile([P, S // 16], U16, name="place")
@@ -41,23 +42,21 @@ def tile_list_tabscat_l_none_kernel(tc, tab, w4_words, w4_scales, down, up, wgo,
         tab_sc = keep.tile([P, PASSES, T], U8, name="tab_sc", align_bytes=64)
         w4_sc = keep.tile([P, PASSES, M], U8, name="w4_sc", align_bytes=64)
         nc.vector.memset(tab_sc[:].bitcast(I32), 0)
-        nc.vector.memset(w4_sc[:].bitcast(I32), 0)
+        nc.gpsimd.memset(w4_sc[:].bitcast(I32), 0)
         tab_sc_rows = tab[:, K_PASS * T :].rearrange("a (q r t) -> r q a t", q=4, r=4)
-        for r in range(4):
-            nc.scalar.dma_start(tab_sc[r:P:32, :, :].bitcast(I32), tab_sc_rows[r].bitcast(I32))
         windows = [keep.tile([P, T], F32, name="window%d" % i) for i in range(WINDOWS)]
-        for w in windows:
+        for w in windows[: WINDOWS // 2]:
             nc.vector.memset(w[:], 0.0)
+        for w in windows[WINDOWS // 2 :]:
+            nc.gpsimd.memset(w[:], 0.0)
 
         down_raw = {}
         tab_w = {}
 
         def load_down(a):
-            for b in range(2):
-                t = keep.tile([P, PACK, R // 2], F32, name="down_raw%d_%d" % (a, b))
-                rows = down[a * K_PASS : (a + 1) * K_PASS, b * (R // 2) : (b + 1) * (R // 2)]
-                nc.sync.dma_start(t[:], rows.rearrange("(p j) c -> p j c", j=PACK))
-                down_raw[(a, b)] = t
+            t = keep.tile([P, PACK, R], F32, name="down_raw%d" % a)
+            nc.sync.dma_start(t[:], down[a * K_PASS : (a + 1) * K_PASS, :].rearrange("(p j) c -> p j c", j=PACK))
+            down_raw[a] = t
 
         def load_tab(a):
             t = keep.tile([P, T], U32, name="tab_w%d" % a, align_bytes=64)
@@ -77,28 +76,31 @@ def tile_list_tabscat_l_none_kernel(tc, tab, w4_words, w4_scales, down, up, wgo,
         def load_w4(lo, hi):
             t = keep.tile([P, PASSES, (hi - lo) * 2 * P], U8, name="w4_w%d" % lo, align_bytes=64)
             src = w4_words[:, :, lo * 2 * P : hi * 2 * P].rearrange("a p w -> p a w")
+            rows = w4_scales[:, :, lo * P : hi * P].rearrange("a (q r) n -> r q a n", r=4)
+            for r in range(4):
+                nc.sync.dma_start(w4_sc[r:P:32, :, lo * P : hi * P].bitcast(I32), rows[r].bitcast(I32))
             nc.sync.dma_start(t[:].bitcast(I32), src.bitcast(I32))
             for i in range(lo, hi):
                 w4_w[i] = (t, (i - lo) * 2 * P)
 
         load_down(0)
-        load_tab(0)
+        for r in range(4):
+            nc.sync.dma_start(tab_sc[r:P:32, :, :].bitcast(I32), tab_sc_rows[r].bitcast(I32))
         load_down(1)
+        load_tab(0)
+        nc.sync.dma_start(place[:], offs2)
         load_tab(1)
         load_tab(2)
         load_down(2)
         load_up(*UP_GROUPS[0])
-        w4_sc_rows = w4_scales.rearrange("a (q r) n -> r q a n", r=4)
-        for r in range(4):
-            nc.sync.dma_start(w4_sc[r:P:32, :, :].bitcast(I32), w4_sc_rows[r].bitcast(I32))
         load_w4(*W4_GROUPS[0])
-        load_up(*UP_GROUPS[1])
         weight = keep.tile([P, S], F32, name="weight")
         nc.sync.dma_start(weight[:], wgo)
-        nc.sync.dma_start(place[:], offs2)
+        load_up(*UP_GROUPS[1])
         load_up(*UP_GROUPS[2])
-        load_w4(*W4_GROUPS[1])
         load_up(*UP_GROUPS[3])
+        load_w4(*W4_GROUPS[1])
+        load_up(*UP_GROUPS[4])
 
         got_w = [keep.tile([P, S], U32, name="got_w%d" % a, align_bytes=64) for a in range(PASSES)]
         got_sc = [keep.tile([P, S], U8, name="got_sc%d" % a, align_bytes=64) for a in range(PASSES)]
@@ -126,47 +128,43 @@ def tile_list_tabscat_l_none_kernel(tc, tab, w4_words, w4_scales, down, up, wgo,
                     stop=(a == PASSES - 1 and t == PACK - 1),
                 )
 
-        HM = P // 2
+        woven = [keep.tile([P, PACK, P, PACK], BF16, name="down_bf%d" % a, align_bytes=64) for a in range(PASSES)]
         for a in range(PASSES - 1):
-            nc.vector.tensor_copy(got_w[a][:], tab_w[a][:].indirect(pick[:]))
-            woven = keep.tile([P, PACK, P, PACK], BF16, name="down_bf%d" % a, align_bytes=64)
-            for b in range(2):
-                weave_down(nc.scalar.copy, woven[:, :, b * HM : (b + 1) * HM, :], down_raw[(a, b)][:])
+            weave_down(nc.scalar.copy, woven[a][:], down_raw[a][:])
             nc.vector.quantize_mx(
-                out=down_q[a][:].bitcast(FP8X4), scales=down_sc[a][:], in_=woven[:].rearrange("p t m j -> p (t m j)")
+                out=down_q[a][:].bitcast(FP8X4), scales=down_sc[a][:], in_=woven[a][:].rearrange("p t m j -> p (t m j)")
             )
+            nc.vector.tensor_copy(got_w[a][:], tab_w[a][:].indirect(pick[:]))
             for t in range(PACK):
                 h_passes(a, t)
         a = PASSES - 1
         nc.vector.tensor_copy(got_w[a][:], tab_w[a][:].indirect(pick[:]))
-        halves = [keep.tile([P, PACK, HM, PACK], BF16, name="down_last%d" % b, align_bytes=64) for b in range(2)]
-        for b in range(2):
-            weave_down(nc.vector.tensor_copy, halves[b][:], down_raw[(a, b)][:])
-            for t in range(PACK):
-                cols = slice(t * P + b * HM, t * P + (b + 1) * HM)
-                nc.vector.quantize_mx(
-                    out=down_q[a][:, cols].bitcast(FP8X4),
-                    scales=down_sc[a][:, cols],
-                    in_=halves[b][:, t, :, :].rearrange("p m j -> p (m j)"),
-                )
+        weave_down(nc.scalar.copy, woven[a][:, :, :SCALAR_SHARE, :], down_raw[a][:, :, : SCALAR_SHARE * PACK])
+        weave_down(nc.vector.tensor_copy, woven[a][:, :, SCALAR_SHARE:, :], down_raw[a][:, :, SCALAR_SHARE * PACK :])
         for t in range(PACK):
+            cols = slice(t * P, (t + 1) * P)
+            nc.vector.quantize_mx(
+                out=down_q[a][:, cols].bitcast(FP8X4),
+                scales=down_sc[a][:, cols],
+                in_=woven[a][:, t, :, :].rearrange("p m j -> p (m j)"),
+            )
             h_passes(a, t)
 
         up_q = {}
 
-        def weave_up(i):
-            woven = keep.tile([P, P, PACK], BF16, name="up_bf%d" % i, align_bytes=64)
+        def prepare_up(i, flat_tag, codes_tag):
+            flat = keep.tile([P, P, PACK], BF16, name=flat_tag, align_bytes=64)
             nc.scalar.copy(
-                woven[:].rearrange("p (c i) j -> p c j i", i=4), up_raw[i].rearrange("p j (c i) -> p c j i", i=4)
+                flat[:].rearrange("p (c i) j -> p c j i", i=4), up_raw[i].rearrange("p j (c i) -> p c j i", i=4)
             )
-            codes = keep.tile([P, P], U32, name="up_q%d" % i, align_bytes=64)
+            codes = keep.tile([P, P], U32, name=codes_tag, align_bytes=64)
             scales = keep.tile([P, P], U8, name="up_sc%d" % i, align_bytes=64)
             nc.vector.quantize_mx(
-                out=codes[:].bitcast(FP8X4), scales=scales[:], in_=woven[:].rearrange("p c j -> p (c j)")
+                out=codes[:].bitcast(FP8X4), scales=scales[:], in_=flat[:].rearrange("p c j -> p (c j)")
             )
-            up_q[i] = (codes, scales)
+            up_q[i] = (codes[:], scales[:])
 
-        weave_up(0)
+        prepare_up(0, "up_bf0", "up_slot")
 
         h_q = keep.tile([P, S], U32, name="h_q", align_bytes=64)
         h_sc = keep.tile([P, S], U8, name="h_sc", align_bytes=64)
@@ -179,36 +177,55 @@ def tile_list_tabscat_l_none_kernel(tc, tab, w4_words, w4_scales, down, up, wgo,
                 out=h_q[:, pos].bitcast(FP8X4), scales=h_sc[:, pos], in_=h_bf[b][:].rearrange("p s t -> p (s t)")
             )
 
-        weave_up(1)
-        for i in range(N_TILES):
-            acc = psum_y.tile([P, S], F32, name="acc")
+        def w4_pass(acc, i, a, b, start):
             words, at = w4_w[i]
-            for a in range(PASSES):
-                for b in range(2):
-                    pos = slice(b * HALF, (b + 1) * HALF)
-                    nc.tensor.matmul_mx(
-                        out=acc[:, pos],
-                        lhsT=words[:, a, at : at + 2 * P].bitcast(FP4X4),
-                        lhsT_scale=w4_sc[:, a, i * P : (i + 1) * P],
-                        rhs=got_w[a][:, pos].bitcast(FP8X4),
-                        rhs_scale=got_sc[a][:, pos],
-                        start=(a == 0 and b == 0),
-                        stop=False,
-                    )
+            pos = slice(b * HALF, (b + 1) * HALF)
+            nc.tensor.matmul_mx(
+                out=acc,
+                lhsT=words[:, a, at : at + 2 * P].bitcast(FP4X4),
+                lhsT_scale=w4_sc[:, a, i * P : (i + 1) * P],
+                rhs=got_w[a][:, pos].bitcast(FP8X4),
+                rhs_scale=got_sc[a][:, pos],
+                start=start,
+                stop=False,
+            )
+
+        def up_pass(acc, i, pos):
             codes, scales = up_q[i]
             nc.tensor.matmul_mx(
-                out=acc[:],
-                lhsT=codes[:].bitcast(FP8X4),
-                lhsT_scale=scales[:],
-                rhs=h_q[:].bitcast(FP8X4),
-                rhs_scale=h_sc[:],
+                out=acc,
+                lhsT=codes.bitcast(FP8X4),
+                lhsT_scale=scales,
+                rhs=h_q[:, pos].bitcast(FP8X4),
+                rhs_scale=h_sc[:, pos],
                 start=False,
                 stop=True,
             )
+
+        accs = [psum_h.tile([P, HALF], F32, name="first%d" % b) for b in range(2)]
+        for b in range(2):
+            for a in range(PASSES):
+                w4_pass(accs[b][:], 0, a, b, a == 0)
+            up_pass(accs[b][:], 0, slice(b * HALF, (b + 1) * HALF))
+        for b in range(2):
+            pos = slice(b * HALF, (b + 1) * HALF)
+            part = keep.tile([P, HALF], F32, name=("y_first", "up_raw1")[b])
+            nc.scalar.copy(part[:], accs[b][:])
+            cols = slice(b * HALF // 16, (b + 1) * HALF // 16)
+            nc.vector.tensor_tensor(windows[0][:].indirect(place[:, cols]), part[:], weight[:, pos], MULT)
+            prepare_up(1 + b, "up_slot", "up_q%d" % (1 + b))
+        nc.sync.dma_start(out[0:P, :], windows[0][:])
+
+        for i in range(1, N_TILES):
+            acc = psum_y.tile([P, S], F32, name="acc")
+            for a in range(PASSES):
+                for b in range(2):
+                    w4_pass(acc[:, b * HALF : (b + 1) * HALF], i, a, b, a == 0 and b == 0)
+            up_pass(acc[:], i, slice(0, S))
             y = ring.tile([P, S], F32, name="y")
             nc.scalar.copy(y[:], acc[:])
-            if i + 2 < N_TILES:
-                weave_up(i + 2)
             window = windows[i % WINDOWS]
             nc.vector.tensor_tensor(window[:].indirect(place[:]), y[:], weight[:], MULT)
             nc.sync.dma_start(out[i * P : (i + 1) * P, :], window[:])
+            if i + 2 < N_TILES:
+                prepare_up(i + 2, "up_slot", "up_q%d" % (i + 2))

@@ -112,7 +112,10 @@ def tile_list_tabscat_l_none_kernel(tc, tab, w4_words, w4_scales, down, up, wgo,
         down_sc = [keep.tile([P, R], U8, name="down_sc%d" % a, align_bytes=64) for a in range(PASSES)]
 
         def weave_down(copy, dst, raw):
-            copy(dst.rearrange("p t m j -> p m j t"), raw.rearrange("p j (m t) -> p m j t", t=PACK))
+            copy(
+                dst.rearrange("p (u v) m j -> p u m j v", v=2),
+                raw.rearrange("p j (m u v) -> p u m j v", u=2, v=2),
+            )
 
         def h_passes(a, t):
             cols = slice(t * P, (t + 1) * P)

@@ -21,8 +21,8 @@ K_PASS = P * PACK
 PASSES = K // K_PASS
 HALF = S // 2
 N_TILES = M // P
-WINDOWS = 6
-SCALAR_SHARE = 44
+WINDOWS = 5
+SCALAR_SHARE = 52
 UP_GROUPS = [(0, 1), (1, 2), (2, 3), (3, 5), (5, 8)]
 W4_GROUPS = [(0, 4), (4, 8)]
 
@@ -37,18 +37,18 @@ def tile_list_tabscat_l_none_kernel(tc, tab, w4_words, w4_scales, down, up, wgo,
 
         pick = keep.tile([P, S // 16], U16, name="pick")
         place = keep.tile([P, S // 16], U16, name="place")
-        nc.sync.dma_start(pick[:], offs)
 
         tab_sc = keep.tile([P, PASSES, T], U8, name="tab_sc", align_bytes=64)
         w4_sc = keep.tile([P, PASSES, M], U8, name="w4_sc", align_bytes=64)
         nc.vector.memset(tab_sc[:].bitcast(I32), 0)
         nc.gpsimd.memset(w4_sc[:].bitcast(I32), 0)
+        w4_sc_rows = w4_scales.rearrange("a (q r) n -> r q a n", r=4)
+        for r in range(4):
+            nc.gpsimd.dma_start(w4_sc[r:P:32, :, :].bitcast(I32), w4_sc_rows[r].bitcast(I32))
         tab_sc_rows = tab[:, K_PASS * T :].rearrange("a (q r t) -> r q a t", q=4, r=4)
         windows = [keep.tile([P, T], F32, name="window%d" % i) for i in range(WINDOWS)]
-        for w in windows[: WINDOWS // 2]:
+        for w in windows:
             nc.vector.memset(w[:], 0.0)
-        for w in windows[WINDOWS // 2 :]:
-            nc.gpsimd.memset(w[:], 0.0)
 
         down_raw = {}
         tab_w = {}
@@ -76,22 +76,20 @@ def tile_list_tabscat_l_none_kernel(tc, tab, w4_words, w4_scales, down, up, wgo,
         def load_w4(lo, hi):
             t = keep.tile([P, PASSES, (hi - lo) * 2 * P], U8, name="w4_w%d" % lo, align_bytes=64)
             src = w4_words[:, :, lo * 2 * P : hi * 2 * P].rearrange("a p w -> p a w")
-            rows = w4_scales[:, :, lo * P : hi * P].rearrange("a (q r) n -> r q a n", r=4)
-            for r in range(4):
-                nc.sync.dma_start(w4_sc[r:P:32, :, lo * P : hi * P].bitcast(I32), rows[r].bitcast(I32))
             nc.sync.dma_start(t[:].bitcast(I32), src.bitcast(I32))
             for i in range(lo, hi):
                 w4_w[i] = (t, (i - lo) * 2 * P)
 
         load_down(0)
+        nc.sync.dma_start(pick[:], offs)
         for r in range(4):
             nc.sync.dma_start(tab_sc[r:P:32, :, :].bitcast(I32), tab_sc_rows[r].bitcast(I32))
         load_down(1)
         load_tab(0)
         nc.sync.dma_start(place[:], offs2)
         load_tab(1)
-        load_tab(2)
         load_down(2)
+        load_tab(2)
         load_up(*UP_GROUPS[0])
         load_w4(*W4_GROUPS[0])
         weight = keep.tile([P, S], F32, name="weight")
@@ -117,19 +115,22 @@ def tile_list_tabscat_l_none_kernel(tc, tab, w4_words, w4_scales, down, up, wgo,
                 raw.rearrange("p j (m u v) -> p u m j v", u=2, v=2),
             )
 
-        def h_passes(a, t):
+        def h_pass(a, t, b):
             cols = slice(t * P, (t + 1) * P)
-            for b in range(2):
-                pos = slice(b * HALF, (b + 1) * HALF)
-                nc.tensor.matmul_mx(
-                    out=h_banks[b][:, t, :],
-                    lhsT=down_q[a][:, cols].bitcast(FP8X4),
-                    lhsT_scale=down_sc[a][:, cols],
-                    rhs=got_w[a][:, pos].bitcast(FP8X4),
-                    rhs_scale=got_sc[a][:, pos],
-                    start=(a == 0 and t == 0),
-                    stop=(a == PASSES - 1 and t == PACK - 1),
-                )
+            pos = slice(b * HALF, (b + 1) * HALF)
+            nc.tensor.matmul_mx(
+                out=h_banks[b][:, t, :],
+                lhsT=down_q[a][:, cols].bitcast(FP8X4),
+                lhsT_scale=down_sc[a][:, cols],
+                rhs=got_w[a][:, pos].bitcast(FP8X4),
+                rhs_scale=got_sc[a][:, pos],
+                start=(a == 0 and t == 0),
+                stop=(a == PASSES - 1 and t == PACK - 1),
+            )
+
+        def gather_half(a, b):
+            cols = slice(b * HALF // 16, (b + 1) * HALF // 16)
+            nc.vector.tensor_copy(got_w[a][:, b * HALF : (b + 1) * HALF], tab_w[a][:].indirect(pick[:, cols]))
 
         woven = [keep.tile([P, PACK, P, PACK], BF16, name="down_bf%d" % a, align_bytes=64) for a in range(PASSES)]
         for a in range(PASSES - 1):
@@ -139,11 +140,12 @@ def tile_list_tabscat_l_none_kernel(tc, tab, w4_words, w4_scales, down, up, wgo,
             )
             nc.vector.tensor_copy(got_w[a][:], tab_w[a][:].indirect(pick[:]))
             for t in range(PACK):
-                h_passes(a, t)
+                for b in range(2):
+                    h_pass(a, t, b)
         a = PASSES - 1
-        nc.vector.tensor_copy(got_w[a][:], tab_w[a][:].indirect(pick[:]))
         weave_down(nc.scalar.copy, woven[a][:, :, :SCALAR_SHARE, :], down_raw[a][:, :, : SCALAR_SHARE * PACK])
         weave_down(nc.vector.tensor_copy, woven[a][:, :, SCALAR_SHARE:, :], down_raw[a][:, :, SCALAR_SHARE * PACK :])
+        gather_half(a, 0)
         for t in range(PACK):
             cols = slice(t * P, (t + 1) * P)
             nc.vector.quantize_mx(
@@ -151,7 +153,10 @@ def tile_list_tabscat_l_none_kernel(tc, tab, w4_words, w4_scales, down, up, wgo,
                 scales=down_sc[a][:, cols],
                 in_=woven[a][:, t, :, :].rearrange("p m j -> p (m j)"),
             )
-            h_passes(a, t)
+            h_pass(a, t, 0)
+        gather_half(a, 1)
+        for t in range(PACK):
+            h_pass(a, t, 1)
 
         up_q = {}
 
@@ -172,9 +177,8 @@ def tile_list_tabscat_l_none_kernel(tc, tab, w4_words, w4_scales, down, up, wgo,
         h_q = keep.tile([P, S], U32, name="h_q", align_bytes=64)
         h_sc = keep.tile([P, S], U8, name="h_sc", align_bytes=64)
         h_bf = [keep.tile([P, HALF, PACK], BF16, name="h_bf%d" % b, align_bytes=64) for b in range(2)]
-        nc.scalar.copy(h_bf[0][:], h_banks[0][:].rearrange("p t s -> p s t"))
-        nc.vector.tensor_copy(h_bf[1][:], h_banks[1][:].rearrange("p t s -> p s t"))
         for b in range(2):
+            nc.scalar.copy(h_bf[b][:], h_banks[b][:].rearrange("p t s -> p s t"))
             pos = slice(b * HALF, (b + 1) * HALF)
             nc.vector.quantize_mx(
                 out=h_q[:, pos].bitcast(FP8X4), scales=h_sc[:, pos], in_=h_bf[b][:].rearrange("p s t -> p (s t)")
@@ -205,7 +209,7 @@ def tile_list_tabscat_l_none_kernel(tc, tab, w4_words, w4_scales, down, up, wgo,
                 stop=True,
             )
 
-        accs = [psum_h.tile([P, HALF], F32, name="first%d" % b) for b in range(2)]
+        accs = [psum_y.tile([P, HALF], F32, name="acc") for b in range(2)]
         for b in range(2):
             for a in range(PASSES):
                 w4_pass(accs[b][:], 0, a, b, a == 0)

from contextlib import ExitStack

import concourse.mybir as mybir

K, M, T, S, R = 1536, 1024, 512, 256, 512
FLOPS = 2 * S * (K * R + K * M + R * M)

F32 = mybir.dt.float32
BF16 = mybir.dt.bfloat16
I32 = mybir.dt.int32
U32 = mybir.dt.uint32
U16 = mybir.dt.uint16
U8 = mybir.dt.uint8
FP8X4 = mybir.dt.float8_e4m3fn_x4
FP4X4 = mybir.dt.float4_e2m1fn_x4
MULT = mybir.AluOpType.mult

P = 128
PACK = 4
K_PASS = P * PACK
PASSES = K // K_PASS
HALF = S // 2
N_TILES = M // P
WINDOWS = 5
SCALAR_SHARE = 52
UP_GROUPS = [(0, 1), (1, 2), (2, 3), (3, 5), (5, 8)]
W4_GROUPS = [(0, 4), (4, 8)]


def tile_list_tabscat_l_none_kernel(tc, tab, w4_words, w4_scales, down, up, wgo, offs, offs2, out):
    nc = tc.nc
    with ExitStack() as ctx:
        keep = ctx.enter_context(tc.tile_pool(name="keep", bufs=1))
        ring = ctx.enter_context(tc.tile_pool(name="ring", bufs=3))
        psum_h = ctx.enter_context(tc.psum_pool(name="psum_h", bufs=1))
        psum_y = ctx.enter_context(tc.psum_pool(name="psum_y", bufs=2))

        pick = keep.tile([P, S // 16], U16, name="pick")
        place = keep.tile([P, S // 16], U16, name="place")

        tab_sc = keep.tile([P, PASSES, T], U8, name="tab_sc", align_bytes=64)
        w4_sc = keep.tile([P, PASSES, M], U8, name="w4_sc", align_bytes=64)
        nc.vector.memset(tab_sc[:].bitcast(I32), 0)
        nc.gpsimd.memset(w4_sc[:].bitcast(I32), 0)
        w4_sc_rows = w4_scales.rearrange("a (q r) n -> r q a n", r=4)
        for r in range(4):
            nc.gpsimd.dma_start(w4_sc[r:P:32, :, :].bitcast(I32), w4_sc_rows[r].bitcast(I32))
        tab_sc_rows = tab[:, K_PASS * T :].rearrange("a (q r t) -> r q a t", q=4, r=4)
        windows = [keep.tile([P, T], F32, name="window%d" % i) for i in range(WINDOWS)]
        for w in windows:
            nc.vector.memset(w[:], 0.0)

        down_raw = {}
        tab_w = {}

        def load_down(a):
            t = keep.tile([P, PACK, R], F32, name="down_raw%d" % a)
            nc.sync.dma_start(t[:], down[a * K_PASS : (a + 1) * K_PASS, :].rearrange("(p j) c -> p j c", j=PACK))
            down_raw[a] = t

        def load_tab(a):
            t = keep.tile([P, T], U32, name="tab_w%d" % a, align_bytes=64)
            nc.sync.dma_start(t[:].bitcast(I32), tab[a, : K_PASS * T].rearrange("(p w) -> p w", p=P).bitcast(I32))
            tab_w[a] = t

        up_raw = {}

        def load_up(lo, hi):
            t = keep.tile([P, PACK, (hi - lo) * P], F32, name="up_raw%d" % lo)
            nc.sync.dma_start(t[:], up[:, lo * P : hi * P].rearrange("(p j) c -> p j c", j=PACK))
            for i in range(lo, hi):
                up_raw[i] = t[:, :, (i - lo) * P : (i - lo + 1) * P]

        w4_w = {}

        def load_w4(lo, hi):
            t = keep.tile([P, PASSES, (hi - lo) * 2 * P], U8, name="w4_w%d" % lo, align_bytes=64)
            src = w4_words[:, :, lo * 2 * P : hi * 2 * P].rearrange("a p w -> p a w")
            nc.sync.dma_start(t[:].bitcast(I32), src.bitcast(I32))
            for i in range(lo, hi):
                w4_w[i] = (t, (i - lo) * 2 * P)

        load_down(0)
        nc.sync.dma_start(pick[:], offs)
        for r in range(4):
            nc.sync.dma_start(tab_sc[r:P:32, :, :].bitcast(I32), tab_sc_rows[r].bitcast(I32))
        load_down(1)
        load_tab(0)
        nc.sync.dma_start(place[:], offs2)
        load_tab(1)
        load_down(2)
        load_tab(2)
        load_up(*UP_GROUPS[0])
        load_w4(*W4_GROUPS[0])
        weight = keep.tile([P, S], F32, name="weight")
        nc.sync.dma_start(weight[:], wgo)
        load_up(*UP_GROUPS[1])
        load_up(*UP_GROUPS[2])
        load_up(*UP_GROUPS[3])
        load_w4(*W4_GROUPS[1])
        load_up(*UP_GROUPS[4])

        got_w = [keep.tile([P, S], U32, name="got_w%d" % a, align_bytes=64) for a in range(PASSES)]
        got_sc = [keep.tile([P, S], U8, name="got_sc%d" % a, align_bytes=64) for a in range(PASSES)]
        for a in range(PASSES):
            nc.vector.tensor_copy(got_sc[a][:], tab_sc[:, a, :].indirect(pick[:]))

        h_banks = [psum_h.tile([P, PACK, HALF], F32, name="h_bank%d" % b) for b in range(2)]
        down_q = [keep.tile([P, R], U32, name="down_q%d" % a, align_bytes=64) for a in range(PASSES)]
        down_sc = [keep.tile([P, R], U8, name="down_sc%d" % a, align_bytes=64) for a in range(PASSES)]

        def weave_down(copy, dst, raw):
            copy(
                dst.rearrange("p (u v) m j -> p u m j v", v=2),
                raw.rearrange("p j (m u v) -> p u m j v", u=2, v=2),
            )

        def h_pass(a, t, b):
            cols = slice(t * P, (t + 1) * P)
            pos = slice(b * HALF, (b + 1) * HALF)
            nc.tensor.matmul_mx(
                out=h_banks[b][:, t, :],
                lhsT=down_q[a][:, cols].bitcast(FP8X4),
                lhsT_scale=down_sc[a][:, cols],
                rhs=got_w[a][:, pos].bitcast(FP8X4),
                rhs_scale=got_sc[a][:, pos],
                start=(a == 0 and t == 0),
                stop=(a == PASSES - 1 and t == PACK - 1),
            )

        def gather_half(a, b):
            cols = slice(b * HALF // 16, (b + 1) * HALF // 16)
            nc.vector.tensor_copy(got_w[a][:, b * HALF : (b + 1) * HALF], tab_w[a][:].indirect(pick[:, cols]))

        woven = [keep.tile([P, PACK, P, PACK], BF16, name="down_bf%d" % a, align_bytes=64) for a in range(PASSES)]
        for a in range(PASSES - 1):
            weave_down(nc.scalar.copy, woven[a][:], down_raw[a][:])
            nc.vector.quantize_mx(
                out=down_q[a][:].bitcast(FP8X4), scales=down_sc[a][:], in_=woven[a][:].rearrange("p t m j -> p (t m j)")
            )
            nc.vector.tensor_copy(got_w[a][:], tab_w[a][:].indirect(pick[:]))
            for t in range(PACK):
                for b in range(2):
                    h_pass(a, t, b)
        a = PASSES - 1
        weave_down(nc.scalar.copy, woven[a][:, :, :SCALAR_SHARE, :], down_raw[a][:, :, : SCALAR_SHARE * PACK])
        weave_down(nc.vector.tensor_copy, woven[a][:, :, SCALAR_SHARE:, :], down_raw[a][:, :, SCALAR_SHARE * PACK :])
        gather_half(a, 0)
        for t in range(PACK):
            cols = slice(t * P, (t + 1) * P)
            nc.vector.quantize_mx(
                out=down_q[a][:, cols].bitcast(FP8X4),
                scales=down_sc[a][:, cols],
                in_=woven[a][:, t, :, :].rearrange("p m j -> p (m j)"),
            )
            h_pass(a, t, 0)
        gather_half(a, 1)
        for t in range(PACK):
            h_pass(a, t, 1)

        up_q = {}

        def prepare_up(i, flat_tag, codes_tag):
            flat = keep.tile([P, P, PACK], BF16, name=flat_tag, align_bytes=64)
            nc.scalar.copy(
                flat[:].rearrange("p (c i) j -> p c j i", i=4), up_raw[i].rearrange("p j (c i) -> p c j i", i=4)
            )
            codes = keep.tile([P, P], U32, name=codes_tag, align_bytes=64)
            scales = keep.tile([P, P], U8, name="up_sc%d" % i, align_bytes=64)
            nc.vector.quantize_mx(
                out=codes[:].bitcast(FP8X4), scales=scales[:], in_=flat[:].rearrange("p c j -> p (c j)")
            )
            up_q[i] = (codes[:], scales[:])

        prepare_up(0, "up_bf0", "up_slot")

        h_q = keep.tile([P, S], U32, name="h_q", align_bytes=64)
        h_sc = keep.tile([P, S], U8, name="h_sc", align_bytes=64)
        h_bf = [keep.tile([P, HALF, PACK], BF16, name="h_bf%d" % b, align_bytes=64) for b in range(2)]
        for b in range(2):
            nc.scalar.copy(h_bf[b][:], h_banks[b][:].rearrange("p t s -> p s t"))
            pos = slice(b * HALF, (b + 1) * HALF)
            nc.vector.quantize_mx(
                out=h_q[:, pos].bitcast(FP8X4), scales=h_sc[:, pos], in_=h_bf[b][:].rearrange("p s t -> p (s t)")
            )

        def w4_pass(acc, i, a, b, start):
            words, at = w4_w[i]
            pos = slice(b * HALF, (b + 1) * HALF)
            nc.tensor.matmul_mx(
                out=acc,
                lhsT=words[:, a, at : at + 2 * P].bitcast(FP4X4),
                lhsT_scale=w4_sc[:, a, i * P : (i + 1) * P],
                rhs=got_w[a][:, pos].bitcast(FP8X4),
                rhs_scale=got_sc[a][:, pos],
                start=start,
                stop=False,
            )

        def up_pass(acc, i, pos):
            codes, scales = up_q[i]
            nc.tensor.matmul_mx(
                out=acc,
                lhsT=codes.bitcast(FP8X4),
                lhsT_scale=scales,
                rhs=h_q[:, pos].bitcast(FP8X4),
                rhs_scale=h_sc[:, pos],
                start=False,
                stop=True,
            )

        accs = [psum_y.tile([P, HALF], F32, name="acc") for b in range(2)]
        for b in range(2):
            for a in range(PASSES):
                w4_pass(accs[b][:], 0, a, b, a == 0)
            up_pass(accs[b][:], 0, slice(b * HALF, (b + 1) * HALF))
        for b in range(2):
            pos = slice(b * HALF, (b + 1) * HALF)
            part = keep.tile([P, HALF], F32, name=("y_first", "up_raw1")[b])
            nc.scalar.copy(part[:], accs[b][:])
            cols = slice(b * HALF // 16, (b + 1) * HALF // 16)
            nc.vector.tensor_tensor(windows[0][:].indirect(place[:, cols]), part[:], weight[:, pos], MULT)
            prepare_up(1 + b, "up_slot", "up_q%d" % (1 + b))
        nc.sync.dma_start(out[0:P, :], windows[0][:])

        for i in range(1, N_TILES):
            acc = psum_y.tile([P, S], F32, name="acc")
            for a in range(PASSES):
                for b in range(2):
                    w4_pass(acc[:, b * HALF : (b + 1) * HALF], i, a, b, a == 0 and b == 0)
            up_pass(acc[:], i, slice(0, S))
            y = ring.tile([P, S], F32, name="y")
            nc.scalar.copy(y[:], acc[:])
            window = windows[i % WINDOWS]
            nc.vector.tensor_tensor(window[:].indirect(place[:]), y[:], weight[:], MULT)
            nc.sync.dma_start(out[i * P : (i + 1) * P, :], window[:])
            if i + 2 < N_TILES:
                prepare_up(i + 2, "up_slot", "up_q%d" % (i + 2))
